import numpy as np
import ml_dtypes


def mxq(x, axis, fmt="e4m3"):
    dtype, down = {"e4m3": (ml_dtypes.float8_e4m3fn, 7), "e5m2": (ml_dtypes.float8_e5m2, 14)}[fmt]
    v = np.moveaxis(np.asarray(x, np.float32).astype(ml_dtypes.bfloat16).astype(np.float64), axis, -1)
    blocks = v.reshape(v.shape[:-1] + (-1, 32))
    amax = np.abs(blocks).max(-1, keepdims=True)
    byte = np.maximum(np.where(amax > 0, np.frexp(amax)[1] - 1 + 127, 0) - down, 1)
    scale = np.exp2(byte - 127.0)
    codes = (blocks / scale).astype(np.float32).astype(dtype).astype(np.float64)
    return np.moveaxis((codes * scale).reshape(v.shape), -1, axis)


WIDE = False


def mx_kscale(k):
    if not WIDE:
        return np.ones(k)
    levels = np.array([10, -10, 5, -5, 0])
    if k % 512:
        return np.exp2(np.random.permutation(np.resize(levels, k // 32))).repeat(32)
    a = np.empty((k // 512, 16))
    for p in range(k // 512):
        a[p, :8] = np.random.permutation(np.resize(levels, 8))
        for g in range(8):
            far = levels[np.abs(levels - a[p, g]) >= 10]
            a[p, g + 8] = far[np.random.randint(len(far))]
    return np.exp2(a.ravel()).repeat(32)


def f64(x):
    return np.asarray(x).astype(np.float64)


def striped(idx):
    return np.tile(np.asarray(idx).reshape(-1, 16).T, (8, 1)).astype(np.uint16)


def unstriped(offs):
    return offs[:16].T.reshape(-1).astype(np.int64)


def striped8(idx):
    return np.asarray(idx).reshape(8, -1, 16).transpose(0, 2, 1).reshape(128, -1).astype(np.uint16)


def unstriped8(offs):
    return offs.reshape(8, 16, -1).transpose(0, 2, 1).reshape(8, -1).astype(np.int64)


def pick8(x, idx, run):
    r = np.arange(len(x))
    return x[r[:, None], idx[r % (8 * run) // run]]


E2M1 = np.array([0.0, 0.5, 1.0, 1.5, 2.0, 3.0, 4.0, 6.0, -0.0, -0.5, -1.0, -1.5, -2.0, -3.0, -4.0, -6.0])


def pack_weight(w, fmt):
    k, n = w.shape
    w = f64(np.asarray(w, np.float32).astype(ml_dtypes.bfloat16)).reshape(k // 32, 32, n)
    amax = np.abs(w).max(1)
    if fmt == "e4m3":
        byte = np.frexp(amax)[1] - 1 + 127 - 7
    else:
        mant, ex = np.frexp(amax / 6.0)
        byte = np.where(mant > 0.5, ex, ex - 1) + 127
    byte = np.clip(np.where(amax > 0, byte, 1), 1, 254)
    scaled = (w * np.exp2(127.0 - byte)[:, None, :]).reshape(k, n).astype(np.float32)
    by_word = np.ascontiguousarray(scaled.reshape(k // 512, 128, 4, n).transpose(0, 1, 3, 2))
    if fmt == "e4m3":
        words = by_word.astype(ml_dtypes.float8_e4m3fn).view(np.uint8)
    else:
        c = by_word.astype(ml_dtypes.float4_e2m1fn).view(np.uint8) & 0xF
        words = (c[..., 0::2] | (c[..., 1::2] << 4)).reshape(k // 512, 128, 2 * n)
    return np.ascontiguousarray(words), np.ascontiguousarray(byte.astype(np.uint8).reshape(k // 512, 16, n))


def unpack_weight(words, scales, fmt):
    g, _, n = scales.shape
    words = np.ascontiguousarray(words).reshape(g, 128, n, -1)
    if fmt == "e4m3":
        vals = words.view(ml_dtypes.float8_e4m3fn).astype(np.float64)
    else:
        nib = np.empty((g, 128, n, 4), np.uint8)
        nib[..., 0::2] = words & 0xF
        nib[..., 1::2] = words >> 4
        vals = E2M1[nib]
    vals = vals * np.repeat(np.exp2(scales.astype(np.float64) - 127.0), 8, axis=1)[..., None]
    return vals.transpose(0, 1, 3, 2).reshape(g * 512, n)


K, J, R, T, U, Z, M, O, N, S = 512, 256, 512, 512, 512, 512, 1024, 128, 256, 512


def setup_inputs():
    n = np.random.standard_normal
    idx = np.stack([np.random.permutation(T)[:J] for _ in range(8)])
    idx2 = np.stack([np.random.permutation(U)[:J] for _ in range(8)])
    idx3 = np.stack([np.random.permutation(U)[:J] for _ in range(8)])
    idx4 = np.random.permutation(M)[:J]
    idx5 = np.stack([np.random.permutation(J)[:O] for _ in range(8)])
    idx6 = np.stack([np.random.permutation(J)[:O] for _ in range(8)])
    idx7 = np.stack([np.random.permutation(S)[:N] for _ in range(8)])
    fk = mx_kscale(K)
    fr = mx_kscale(R)
    fz = mx_kscale(Z)
    wp = pack_weight(n((K, R)) * 1 / np.sqrt(K) / fk[:, None] * fr, "e2m1")
    xop = pack_weight(n((Z, M)) / fz[:, None], "e2m1")
    w2p = pack_weight(n((Z, R)) * 1 / np.sqrt(Z) * fz[:, None] * fr, "e4m3")
    return {
        "ta": (np.random.randint(-7, 8, (K, T)).astype(np.float64)).astype(np.float32),
        "ga": ((np.random.randint(8, 25, (K, 1)) / 64.0) * fk[:, None]).astype(np.float32),
        "gb": (np.random.uniform(0.5, 1.6, (K, 1))).astype(np.float32),
        "w_words": wp[0],
        "w_scales": wp[1],
        "xo_words": xop[0],
        "xo_scales": xop[1],
        "w2_words": w2p[0],
        "w2_scales": w2p[1],
        "sa": (np.random.uniform(0.5, 1.6, (R, 1))).astype(np.float32),
        "sb": (np.random.uniform(0.5, 1.6, (R, 1))).astype(np.float32),
        "va": (np.random.randint(-7, 8, (R, S)).astype(np.float64)).astype(np.float32),
        "ea": ((np.random.randint(8, 25, (R, 1)) / 1024.0) / fr[:, None]).astype(np.float32),
        "offs": striped8(idx),
        "offs2": striped8(idx2),
        "offs3": striped8(idx3),
        "offs4": striped(idx4),
        "offs5": striped8(idx5),
        "offs6": striped8(idx6),
        "offs7": striped8(idx7),
    }


def reference(ta, ga, gb, w_words, w_scales, xo_words, xo_scales, w2_words, w2_scales, sa, sb, va, ea, offs, offs2, offs3, offs4, offs5, offs6, offs7):
    idx = unstriped8(offs)
    idx2 = unstriped8(offs2)
    idx3 = unstriped8(offs3)
    idx4 = unstriped(offs4)
    idx5 = unstriped8(offs5)
    idx6 = unstriped8(offs6)
    idx7 = unstriped8(offs7)
    wu = unpack_weight(w_words, w_scales, "e2m1")
    xou = unpack_weight(xo_words, xo_scales, "e2m1")
    w2u = unpack_weight(w2_words, w2_scales, "e4m3")
    xcd = pick8(f64(ta), idx, 64) * f64(ga)
    xcp = np.zeros((K, U))
    xcp[np.arange(K)[:, None], idx2[np.arange(K) % 512 // 64]] = xcd
    xc = pick8(xcp, idx3, 64) * f64(gb)
    xcq = mxq(xc, 0, "e4m3")
    a = wu.T @ xcq
    xoidx4g = xou[:, idx4]
    b = w2u.T @ xoidx4g
    hid = np.maximum(pick8(a, idx5, 64) * f64(sa), pick8(b, idx6, 64) * f64(sb))
    vc = pick8(f64(va), idx7, 64) * f64(ea)
    vcq = mxq(vc, 0, "e4m3")
    hidq = mxq(hid, 0, "e4m3")
    y = vcq.T @ hidq
    return y

@@ -1,0 +1,217 @@
+from contextlib import ExitStack
+
+import concourse.mybir as mybir
+
+K, J, R, T, U, Z, M, O, N, S = 512, 256, 512, 512, 512, 512, 1024, 128, 256, 512
+FLOPS = 2 * K * R * J + 2 * Z * R * J + 2 * R * N * O
+
+F32 = mybir.dt.float32
+BF16 = mybir.dt.bfloat16
+I32 = mybir.dt.int32
+U32 = mybir.dt.uint32
+U16 = mybir.dt.uint16
+U8 = mybir.dt.uint8
+FP8X4 = mybir.dt.float8_e4m3fn_x4
+FP4X4 = mybir.dt.float4_e2m1fn_x4
+COPY = mybir.ActivationFunctionType.Copy
+MAX = mybir.AluOpType.max
+
+P = 128
+PACK = 4
+HALF = J // 2
+
+
+def tile_picked_codepage_plain_two_groupmeet_codes_plain_kernel(
+    tc, ta, ga, gb, w_words, w_scales, xo_words, xo_scales, w2_words, w2_scales, sa, sb, va, ea,
+    offs, offs2, offs3, offs4, offs5, offs6, offs7, out,
+):
+    nc = tc.nc
+    with ExitStack() as ctx:
+        lists = ctx.enter_context(tc.tile_pool(name="lists", bufs=1))
+        keep = ctx.enter_context(tc.tile_pool(name="keep", bufs=1))
+        psum = ctx.enter_context(tc.psum_pool(name="psum", bufs=1))
+
+        def sb_tile(shape, dtype, name, tag=None):
+            return keep.tile(shape, dtype, name=name, tag=tag or name, align_bytes=64)
+
+        def load_list(src, name):
+            t = lists.tile(list(src.shape), U16, name=name)
+            nc.sync.dma_start(t[:], src)
+            return t
+
+        def load_column(queue, src, name):
+            t = sb_tile([P, PACK], F32, name)
+            queue.dma_start(t[:], src.rearrange("(p t) one -> p (t one)", t=PACK))
+            return t
+
+        def load_rows(src, t, name):
+            tl = sb_tile([P, src.shape[1]], F32, name)
+            nc.sync.dma_start(tl[:], src.rearrange("(p t) c -> t p c", t=PACK)[t])
+            return tl
+
+        def load_scale_rows(queue, src, plane):
+            rows = src[0].bitcast(I32).rearrange("(q i) c -> i q c", i=4)
+            for i in range(4):
+                queue.dma_start(plane[i:P:32, :].bitcast(I32), rows[i])
+
+        def interleave(engine, dst, src):
+            engine.tensor_copy(
+                dst.rearrange("p (c i) t -> p c t i", i=4),
+                src.rearrange("p t (c i) -> p c t i", i=4),
+            )
+
+        xo_plane = sb_tile([P, M], U8, "xo_plane")
+        nc.vector.memset(xo_plane[:].bitcast(I32), 0)
+        page = [sb_tile([P, U], F32, "page%d" % t) for t in range(PACK)]
+        nc.vector.memset(page[0][:], 0.0)
+        nc.vector.memset(page[1][:], 0.0)
+        nc.gpsimd.memset(page[2][:], 0.0)
+        nc.gpsimd.memset(page[3][:], 0.0)
+        w2_plane = sb_tile([P, R], U8, "w2_plane")
+        nc.gpsimd.memset(w2_plane[:].bitcast(I32), 0)
+        w_plane = sb_tile([P, R], U8, "w_plane")
+        nc.gpsimd.memset(w_plane[:].bitcast(I32), 0)
+
+        ta_t = [None] * PACK
+        va_t = [None] * PACK
+        gb_t = load_column(nc.gpsimd, gb, "gb_t")
+        sb_t = load_column(nc.gpsimd, sb, "sb_t")
+        sa_t = load_column(nc.gpsimd, sa, "sa_t")
+        xo_stage = sb_tile([4, 4, M // 4], I32, "xo_stage")
+        nc.sync.dma_start(xo_stage[:], xo_scales[0].bitcast(I32).rearrange("(q i) c -> i q c", i=4))
+        l4 = load_list(offs4, "l4")
+        l1 = load_list(offs, "l1")
+        ga_t = load_column(nc.sync, ga, "ga_t")
+        ta_t[0] = load_rows(ta, 0, "ta0")
+        l2 = load_list(offs2, "l2")
+        ta_t[1] = load_rows(ta, 1, "ta1")
+        ta_t[2] = load_rows(ta, 2, "ta2")
+        va_t[0] = load_rows(va, 0, "va0")
+        l7 = load_list(offs7, "l7")
+        ea_t = load_column(nc.sync, ea, "ea_t")
+        ta_t[3] = load_rows(ta, 3, "ta3")
+        va_t[1] = load_rows(va, 1, "va1")
+        w_w = sb_tile([P, 2 * R], U8, "w_w")
+        nc.sync.dma_start(w_w[:].bitcast(I32), w_words[0].bitcast(I32))
+        va_t[2] = load_rows(va, 2, "va2")
+        w2_w = sb_tile([P, R], U32, "w2_w")
+        nc.sync.dma_start(w2_w[:].bitcast(I32), w2_words[0].rearrange("p n t -> p (n t)").bitcast(I32))
+        va_t[3] = load_rows(va, 3, "va3")
+        xo_w = sb_tile([P, M], U16, "xo_w")
+        nc.sync.dma_start(xo_w[:].bitcast(I32), xo_words[0].bitcast(I32))
+        l3 = load_list(offs3, "l3")
+        load_scale_rows(nc.sync, w2_scales, w2_plane)
+        load_scale_rows(nc.sync, w_scales, w_plane)
+        l6 = load_list(offs6, "l6")
+        l5 = load_list(offs5, "l5")
+
+        for q in range(4):
+            nc.vector.tensor_copy(xo_plane[32 * q : 32 * q + 4, :].bitcast(I32), xo_stage[:, q, :])
+        xo_gs = sb_tile([P, J], U8, "xo_gs")
+        nc.vector.tensor_copy(xo_gs[:], xo_plane[:].indirect(l4[:]))
+
+        w2_dw = sb_tile([P, R], U32, "w2_dw")
+        nc.gpsimd.tensor_copy(w2_dw[:].rearrange("p (t m) -> p t m", t=PACK), w2_w[:].rearrange("p (m t) -> p t m", t=PACK))
+        w2_ds = sb_tile([P, R], U8, "w2_ds")
+        nc.gpsimd.tensor_copy(w2_ds[:].rearrange("p (t m) -> p t m", t=PACK), w2_plane[:].rearrange("p (m t) -> p t m", t=PACK))
+        w_dw = sb_tile([P, 2 * R], U8, "w_dw")
+        nc.gpsimd.tensor_copy(w_dw[:].rearrange("p (t m e) -> p t m e", t=PACK, e=2), w_w[:].rearrange("p (m t e) -> p t m e", t=PACK, e=2))
+        w_ds = sb_tile([P, R], U8, "w_ds")
+        nc.gpsimd.tensor_copy(w_ds[:].rearrange("p (t m) -> p t m", t=PACK), w_plane[:].rearrange("p (m t) -> p t m", t=PACK))
+
+        xcd = [sb_tile([P, J], F32, "xcd%d" % t) for t in range(PACK)]
+        vc_pl = sb_tile([P, PACK, N], BF16, "vc_pl")
+        xo_gw = sb_tile([P, J], U16, "xo_gw")
+
+        def fetch(dst, window, lst, scale):
+            nc.scalar.activation(out=dst, in_=window[:].indirect(lst), func=COPY, scale=scale)
+
+        for t in range(PACK):
+            fetch(xcd[t][:], ta_t[t], l1[:], ga_t[:, t : t + 1])
+            nc.vector.tensor_copy(page[t][:].indirect(l2[:]), xcd[t][:])
+
+        last = PACK - 1
+        for t in range(PACK):
+            fetch(vc_pl[:, t, :], va_t[t], l7[:], ea_t[:, t : t + 1])
+
+        nc.vector.tensor_copy(xo_gw[:], xo_w[:].indirect(l4[:]))
+
+        xc_pl = sb_tile([P, PACK, J], BF16, "xc_pl")
+        for t in range(last):
+            fetch(xc_pl[:, t, :], page[t], l3[:], gb_t[:, t : t + 1])
+        xc_il = sb_tile([P, J, PACK], BF16, "xc_il")
+        xc_q = sb_tile([P, J], U32, "xc_q")
+        xc_s = sb_tile([P, J], U8, "xc_s")
+        for h in range(2):
+            cols = slice(h * HALF, (h + 1) * HALF)
+            lcols = slice(h * HALF // 16, (h + 1) * HALF // 16)
+            fetch(xc_pl[:, last, cols], page[last], l3[:, lcols], gb_t[:, last : last + 1])
+            interleave(nc.vector, xc_il[:, cols, :], xc_pl[:, :, cols])
+        for h in range(2):
+            cols = slice(h * HALF, (h + 1) * HALF)
+            nc.vector.quantize_mx(
+                out=xc_q[:, cols].bitcast(FP8X4), scales=xc_s[:, cols],
+                in_=xc_il[:, cols, :].rearrange("p c t -> p (c t)"),
+            )
+
+        b_sb = [sb_tile([P, J], F32, "b%d" % t) for t in range(PACK)]
+        for t in range(PACK):
+            cols = slice(t * P, (t + 1) * P)
+            acc = psum.tile([P, J], F32, name="b_ps%d" % t, tag="bank%d" % t)
+            nc.tensor.matmul_mx(
+                out=acc[:], lhsT=w2_dw[:, cols].bitcast(FP8X4), lhsT_scale=w2_ds[:, cols],
+                rhs=xo_gw[:].bitcast(FP4X4), rhs_scale=xo_gs[:], start=True, stop=True,
+            )
+            if t == 0:
+                nc.scalar.copy(b_sb[t][:], acc[:])
+            else:
+                nc.vector.tensor_copy(b_sb[t][:], acc[:])
+
+        b_g = sb_tile([P, PACK, O], F32, "b_g", tag="page3")
+        for t in range(PACK):
+            fetch(b_g[:, t, :], b_sb[t], l6[:], sb_t[:, t : t + 1])
+
+        a_ps = [psum.tile([P, J], F32, name="a_ps%d" % t, tag="bank%d" % (PACK + t)) for t in range(PACK)]
+        a_sb = [sb_tile([P, J], F32, "a%d" % t) for t in range(PACK)]
+        a_g = sb_tile([P, PACK, O], F32, "a_g")
+        for t in range(PACK):
+            for h in range(2):
+                cols = slice(h * HALF, (h + 1) * HALF)
+                nc.tensor.matmul_mx(
+                    out=a_ps[t][:, cols], lhsT=w_dw[:, 2 * t * P : 2 * (t + 1) * P].bitcast(FP4X4),
+                    lhsT_scale=w_ds[:, t * P : (t + 1) * P],
+                    rhs=xc_q[:, cols].bitcast(FP8X4), rhs_scale=xc_s[:, cols], start=True, stop=True,
+                )
+            nc.vector.tensor_copy(a_sb[t][:], a_ps[t][:])
+            fetch(a_g[:, t, :], a_sb[t], l5[:], sa_t[:, t : t + 1])
+
+        vc_il = sb_tile([P, N, PACK], BF16, "vc_il", tag="xc_q")
+        interleave(nc.vector, vc_il[:], vc_pl[:])
+
+        hid_il = sb_tile([P, O, PACK], BF16, "hid_il")
+        nc.vector.tensor_tensor(
+            hid_il[:].rearrange("p (c i) t -> p c t i", i=4),
+            a_g[:].rearrange("p t (c i) -> p c t i", i=4),
+            b_g[:].rearrange("p t (c i) -> p c t i", i=4),
+            MAX,
+        )
+        vc_q = sb_tile([P, N], U32, "vc_q")
+        vc_s = sb_tile([P, N], U8, "vc_s")
+        nc.vector.quantize_mx(out=vc_q[:].bitcast(FP8X4), scales=vc_s[:], in_=vc_il[:].rearrange("p c t -> p (c t)"))
+        hid_q = sb_tile([P, O], U32, "hid_q")
+        hid_s = sb_tile([P, O], U8, "hid_s")
+        nc.vector.quantize_mx(out=hid_q[:].bitcast(FP8X4), scales=hid_s[:], in_=hid_il[:].rearrange("p c t -> p (c t)"))
+
+        y_sb = sb_tile([P, 2, O], F32, "y_sb")
+        for h in range(2):
+            cols = slice(h * P, (h + 1) * P)
+            y_ps = psum.tile([P, O], F32, name="y_ps%d" % h, tag="bank%d" % h)
+            nc.tensor.matmul_mx(
+                out=y_ps[:], lhsT=vc_q[:, cols].bitcast(FP8X4), lhsT_scale=vc_s[:, cols],
+                rhs=hid_q[:].bitcast(FP8X4), rhs_scale=hid_s[:], start=True, stop=True,
+            )
+            if h == 0:
+                nc.vector.tensor_copy(y_sb[:, h, :], y_ps[:])
+            else:
+                nc.scalar.copy(y_sb[:, h, :], y_ps[:])
+        nc.sync.dma_start(out.rearrange("(h p) o -> p h o", p=P), y_sb[:])

@@ -60,6 +60,11 @@ def tile_picked_codepage_plain_two_groupmeet_codes_plain_kernel(
                 src.rearrange("p t (c i) -> p c t i", i=4),
             )
 
+        warm_in = sb_tile([P, 1], F32, "warm_in")
+        warm_out = sb_tile([P, 1], F32, "warm_out")
+        nc.gpsimd.memset(warm_in[:], 0.0)
+        nc.scalar.activation(out=warm_out[:], in_=warm_in[:], func=COPY)
+
         xo_plane = sb_tile([P, M], U8, "xo_plane")
         nc.vector.memset(xo_plane[:].bitcast(I32), 0)
         page = [sb_tile([P, U], F32, "page%d" % t) for t in range(PACK)]

@@ -29,6 +29,7 @@ def tile_picked_codepage_plain_two_groupmeet_codes_plain_kernel(
     with ExitStack() as ctx:
         lists = ctx.enter_context(tc.tile_pool(name="lists", bufs=1))
         keep = ctx.enter_context(tc.tile_pool(name="keep", bufs=1))
+        shared = ctx.enter_context(tc.tile_pool(name="shared", bufs=1))
         psum = ctx.enter_context(tc.psum_pool(name="psum", bufs=1))
 
         def sb_tile(shape, dtype, name, tag=None):
@@ -82,36 +83,38 @@ def tile_picked_codepage_plain_two_groupmeet_codes_plain_kernel(
         gb_t = load_column(nc.gpsimd, gb, "gb_t")
         sb_t = load_column(nc.gpsimd, sb, "sb_t")
         sa_t = load_column(nc.gpsimd, sa, "sa_t")
-        xo_stage = sb_tile([4, 4, M // 4], I32, "xo_stage")
-        nc.sync.dma_start(xo_stage[:], xo_scales[0].bitcast(I32).rearrange("(q i) c -> i q c", i=4))
-        l4 = load_list(offs4, "l4")
+        xo_rows = xo_scales[0].bitcast(I32).rearrange("(q i) c -> i q c", i=4)
+        xo_stage = sb_tile([4, 3, M // 4], I32, "xo_stage")
+        nc.sync.dma_start(xo_stage[:], xo_rows[:, 1:4, :])
+        ta_t[0] = load_rows(ta, 0, "ta0")
         l1 = load_list(offs, "l1")
         ga_t = load_column(nc.sync, ga, "ga_t")
-        ta_t[0] = load_rows(ta, 0, "ta0")
+        l4 = load_list(offs4, "l4")
+        nc.sync.dma_start(xo_plane[0:4, :].bitcast(I32), xo_rows[:, 0, :])
         l2 = load_list(offs2, "l2")
         ta_t[1] = load_rows(ta, 1, "ta1")
         ta_t[2] = load_rows(ta, 2, "ta2")
-        va_t[0] = load_rows(va, 0, "va0")
         l7 = load_list(offs7, "l7")
         ea_t = load_column(nc.sync, ea, "ea_t")
+        va_t[0] = load_rows(va, 0, "va0")
         ta_t[3] = load_rows(ta, 3, "ta3")
         va_t[1] = load_rows(va, 1, "va1")
         w_w = sb_tile([P, 2 * R], U8, "w_w")
         nc.sync.dma_start(w_w[:].bitcast(I32), w_words[0].bitcast(I32))
         va_t[2] = load_rows(va, 2, "va2")
+        load_scale_rows(nc.sync, w_scales, w_plane)
+        va_t[3] = load_rows(va, 3, "va3")
+        l3 = load_list(offs3, "l3")
         w2_w = sb_tile([P, R], U32, "w2_w")
         nc.sync.dma_start(w2_w[:].bitcast(I32), w2_words[0].rearrange("p n t -> p (n t)").bitcast(I32))
-        va_t[3] = load_rows(va, 3, "va3")
-        xo_w = sb_tile([P, M], U16, "xo_w")
-        nc.sync.dma_start(xo_w[:].bitcast(I32), xo_words[0].bitcast(I32))
-        l3 = load_list(offs3, "l3")
         load_scale_rows(nc.sync, w2_scales, w2_plane)
-        load_scale_rows(nc.sync, w_scales, w_plane)
+        xo_w = shared.tile([P, M], U16, name="xo_w", align_bytes=64, offset=0)
+        nc.sync.dma_start(xo_w[:].bitcast(I32), xo_words[0].bitcast(I32))
         l6 = load_list(offs6, "l6")
         l5 = load_list(offs5, "l5")
 
-        for q in range(4):
-            nc.vector.tensor_copy(xo_plane[32 * q : 32 * q + 4, :].bitcast(I32), xo_stage[:, q, :])
+        for q in range(1, 4):
+            nc.vector.tensor_copy(xo_plane[32 * q : 32 * q + 4, :].bitcast(I32), xo_stage[:, q - 1, :])
         xo_gs = sb_tile([P, J], U8, "xo_gs")
         nc.vector.tensor_copy(xo_gs[:], xo_plane[:].indirect(l4[:]))
 
@@ -139,12 +142,15 @@ def tile_picked_codepage_plain_two_groupmeet_codes_plain_kernel(
         for t in range(PACK):
             fetch(vc_pl[:, t, :], va_t[t], l7[:], ea_t[:, t : t + 1])
 
-        nc.vector.tensor_copy(xo_gw[:], xo_w[:].indirect(l4[:]))
+        for h in range(2):
+            cols = slice(h * HALF, (h + 1) * HALF)
+            lcols = slice(h * HALF // 16, (h + 1) * HALF // 16)
+            nc.vector.tensor_copy(xo_gw[:, cols], xo_w[:].indirect(l4[:, lcols]))
 
         xc_pl = sb_tile([P, PACK, J], BF16, "xc_pl")
         for t in range(last):
             fetch(xc_pl[:, t, :], page[t], l3[:], gb_t[:, t : t + 1])
-        xc_il = sb_tile([P, J, PACK], BF16, "xc_il")
+        xc_il = shared.tile([P, J, PACK], BF16, name="xc_il", align_bytes=64, offset=0)
         xc_q = sb_tile([P, J], U32, "xc_q")
         xc_s = sb_tile([P, J], U8, "xc_s")
         for h in range(2):
@@ -159,18 +165,23 @@ def tile_picked_codepage_plain_two_groupmeet_codes_plain_kernel(
                 in_=xc_il[:, cols, :].rearrange("p c t -> p (c t)"),
             )
 
-        b_sb = [sb_tile([P, J], F32, "b%d" % t) for t in range(PACK)]
+        b_sb = [sb_tile([P, J], F32, "b%d" % t) for t in range(2)]
+        for t in range(2, PACK):
+            b_sb.append(shared.tile([P, J], F32, name="b%d" % t, align_bytes=64, offset=1024 * (t - 2)))
+        b_ps = [psum.tile([P, J], F32, name="b_ps%d" % t, tag="bank%d" % t) for t in range(PACK)]
+        for h in range(2):
+            cols = slice(h * HALF, (h + 1) * HALF)
+            for t in range(PACK):
+                rows = slice(t * P, (t + 1) * P)
+                nc.tensor.matmul_mx(
+                    out=b_ps[t][:, cols], lhsT=w2_dw[:, rows].bitcast(FP8X4), lhsT_scale=w2_ds[:, rows],
+                    rhs=xo_gw[:, cols].bitcast(FP4X4), rhs_scale=xo_gs[:, cols], start=True, stop=True,
+                )
         for t in range(PACK):
-            cols = slice(t * P, (t + 1) * P)
-            acc = psum.tile([P, J], F32, name="b_ps%d" % t, tag="bank%d" % t)
-            nc.tensor.matmul_mx(
-                out=acc[:], lhsT=w2_dw[:, cols].bitcast(FP8X4), lhsT_scale=w2_ds[:, cols],
-                rhs=xo_gw[:].bitcast(FP4X4), rhs_scale=xo_gs[:], start=True, stop=True,
-            )
-            if t == 0:
-                nc.scalar.copy(b_sb[t][:], acc[:])
+            if t < 2:
+                nc.scalar.copy(b_sb[t][:], b_ps[t][:])
             else:
-                nc.vector.tensor_copy(b_sb[t][:], acc[:])
+                nc.vector.tensor_copy(b_sb[t][:], b_ps[t][:])
 
         b_g = sb_tile([P, PACK, O], F32, "b_g", tag="page3")
         for t in range(PACK):
@@ -217,6 +228,7 @@ def tile_picked_codepage_plain_two_groupmeet_codes_plain_kernel(
             )
             if h == 0:
                 nc.vector.tensor_copy(y_sb[:, h, :], y_ps[:])
+                nc.sync.dma_start(out[cols, :], y_sb[:, h, :])
             else:
                 nc.scalar.copy(y_sb[:, h, :], y_ps[:])
-        nc.sync.dma_start(out.rearrange("(h p) o -> p h o", p=P), y_sb[:])
+                nc.scalar.dma_start(out[cols, :], y_sb[:, h, :])

@@ -69,40 +69,34 @@ def tile_picked_codepage_plain_two_groupmeet_codes_plain_kernel(
         xo_plane = sb_tile([P, M], U8, "xo_plane")
         nc.vector.memset(xo_plane[:].bitcast(I32), 0)
         page = [sb_tile([P, U], F32, "page%d" % t) for t in range(PACK)]
-        nc.vector.memset(page[0][:], 0.0)
-        nc.vector.memset(page[1][:], 0.0)
-        nc.gpsimd.memset(page[2][:], 0.0)
-        nc.gpsimd.memset(page[3][:], 0.0)
-        w2_plane = sb_tile([P, R], U8, "w2_plane")
-        nc.gpsimd.memset(w2_plane[:].bitcast(I32), 0)
+        for t in range(PACK):
+            nc.vector.memset(page[t][:], 0.0)
         w_plane = sb_tile([P, R], U8, "w_plane")
         nc.gpsimd.memset(w_plane[:].bitcast(I32), 0)
+        w2_plane = sb_tile([P, R], U8, "w2_plane")
+        nc.gpsimd.memset(w2_plane[:].bitcast(I32), 0)
 
         ta_t = [None] * PACK
         va_t = [None] * PACK
+        load_scale_rows(nc.gpsimd, w_scales, w_plane)
         gb_t = load_column(nc.gpsimd, gb, "gb_t")
-        sb_t = load_column(nc.gpsimd, sb, "sb_t")
-        sa_t = load_column(nc.gpsimd, sa, "sa_t")
-        xo_rows = xo_scales[0].bitcast(I32).rearrange("(q i) c -> i q c", i=4)
-        xo_stage = sb_tile([4, 3, M // 4], I32, "xo_stage")
-        nc.sync.dma_start(xo_stage[:], xo_rows[:, 1:4, :])
+        xo_stage = sb_tile([4, 4, M // 4], I32, "xo_stage")
+        nc.sync.dma_start(xo_stage[:], xo_scales[0].bitcast(I32).rearrange("(q i) c -> i q c", i=4))
         ta_t[0] = load_rows(ta, 0, "ta0")
         l1 = load_list(offs, "l1")
         ga_t = load_column(nc.sync, ga, "ga_t")
         l4 = load_list(offs4, "l4")
-        nc.sync.dma_start(xo_plane[0:4, :].bitcast(I32), xo_rows[:, 0, :])
         l2 = load_list(offs2, "l2")
         ta_t[1] = load_rows(ta, 1, "ta1")
         ta_t[2] = load_rows(ta, 2, "ta2")
+        va_t[0] = load_rows(va, 0, "va0")
         l7 = load_list(offs7, "l7")
         ea_t = load_column(nc.sync, ea, "ea_t")
-        va_t[0] = load_rows(va, 0, "va0")
         ta_t[3] = load_rows(ta, 3, "ta3")
         va_t[1] = load_rows(va, 1, "va1")
         w_w = sb_tile([P, 2 * R], U8, "w_w")
         nc.sync.dma_start(w_w[:].bitcast(I32), w_words[0].bitcast(I32))
         va_t[2] = load_rows(va, 2, "va2")
-        load_scale_rows(nc.sync, w_scales, w_plane)
         va_t[3] = load_rows(va, 3, "va3")
         l3 = load_list(offs3, "l3")
         w2_w = sb_tile([P, R], U32, "w2_w")
@@ -111,10 +105,12 @@ def tile_picked_codepage_plain_two_groupmeet_codes_plain_kernel(
         xo_w = shared.tile([P, M], U16, name="xo_w", align_bytes=64, offset=0)
         nc.sync.dma_start(xo_w[:].bitcast(I32), xo_words[0].bitcast(I32))
         l6 = load_list(offs6, "l6")
+        sb_t = load_column(nc.sync, sb, "sb_t")
         l5 = load_list(offs5, "l5")
+        sa_t = load_column(nc.sync, sa, "sa_t")
 
-        for q in range(1, 4):
-            nc.vector.tensor_copy(xo_plane[32 * q : 32 * q + 4, :].bitcast(I32), xo_stage[:, q - 1, :])
+        for q in range(4):
+            nc.vector.tensor_copy(xo_plane[32 * q : 32 * q + 4, :].bitcast(I32), xo_stage[:, q, :])
         xo_gs = sb_tile([P, J], U8, "xo_gs")
         nc.vector.tensor_copy(xo_gs[:], xo_plane[:].indirect(l4[:]))
 

@@ -94,7 +94,7 @@ def tile_picked_codepage_plain_two_groupmeet_codes_plain_kernel(
         ea_t = load_column(nc.sync, ea, "ea_t")
         ta_t[3] = load_rows(ta, 3, "ta3")
         va_t[1] = load_rows(va, 1, "va1")
-        w_w = sb_tile([P, 2 * R], U8, "w_w")
+        w_w = sb_tile([P, R], U16, "w_w")
         nc.sync.dma_start(w_w[:].bitcast(I32), w_words[0].bitcast(I32))
         va_t[2] = load_rows(va, 2, "va2")
         va_t[3] = load_rows(va, 3, "va3")
@@ -118,8 +118,6 @@ def tile_picked_codepage_plain_two_groupmeet_codes_plain_kernel(
         nc.gpsimd.tensor_copy(w2_dw[:].rearrange("p (t m) -> p t m", t=PACK), w2_w[:].rearrange("p (m t) -> p t m", t=PACK))
         w2_ds = sb_tile([P, R], U8, "w2_ds")
         nc.gpsimd.tensor_copy(w2_ds[:].rearrange("p (t m) -> p t m", t=PACK), w2_plane[:].rearrange("p (m t) -> p t m", t=PACK))
-        w_dw = sb_tile([P, 2 * R], U8, "w_dw")
-        nc.gpsimd.tensor_copy(w_dw[:].rearrange("p (t m e) -> p t m e", t=PACK, e=2), w_w[:].rearrange("p (m t e) -> p t m e", t=PACK, e=2))
         w_ds = sb_tile([P, R], U8, "w_ds")
         nc.gpsimd.tensor_copy(w_ds[:].rearrange("p (t m) -> p t m", t=PACK), w_plane[:].rearrange("p (m t) -> p t m", t=PACK))
 
@@ -142,6 +140,9 @@ def tile_picked_codepage_plain_two_groupmeet_codes_plain_kernel(
             cols = slice(h * HALF, (h + 1) * HALF)
             lcols = slice(h * HALF // 16, (h + 1) * HALF // 16)
             nc.vector.tensor_copy(xo_gw[:, cols], xo_w[:].indirect(l4[:, lcols]))
+
+        w_dw = sb_tile([P, R], U16, "w_dw")
+        nc.scalar.copy(w_dw[:].rearrange("p (t c i) -> p c t i", t=PACK, i=8), w_w[:].rearrange("p (c i t) -> p c t i", t=PACK, i=8))
 
         xc_pl = sb_tile([P, PACK, J], BF16, "xc_pl")
         for t in range(last):
@@ -190,7 +191,7 @@ def tile_picked_codepage_plain_two_groupmeet_codes_plain_kernel(
             for h in range(2):
                 cols = slice(h * HALF, (h + 1) * HALF)
                 nc.tensor.matmul_mx(
-                    out=a_ps[t][:, cols], lhsT=w_dw[:, 2 * t * P : 2 * (t + 1) * P].bitcast(FP4X4),
+                    out=a_ps[t][:, cols], lhsT=w_dw[:, t * P : (t + 1) * P].bitcast(FP4X4),
                     lhsT_scale=w_ds[:, t * P : (t + 1) * P],
                     rhs=xc_q[:, cols].bitcast(FP8X4), rhs_scale=xc_s[:, cols], start=True, stop=True,
                 )
@@ -224,7 +225,6 @@ def tile_picked_codepage_plain_two_groupmeet_codes_plain_kernel(
             )
             if h == 0:
                 nc.vector.tensor_copy(y_sb[:, h, :], y_ps[:])
-                nc.sync.dma_start(out[cols, :], y_sb[:, h, :])
             else:
                 nc.scalar.copy(y_sb[:, h, :], y_ps[:])
-                nc.scalar.dma_start(out[cols, :], y_sb[:, h, :])
+        nc.sync.dma_start(out.rearrange("(h p) o -> p h o", p=P), y_sb[:])

from contextlib import ExitStack

import concourse.mybir as mybir

K, J, R, T, U, Z, M, O, N, S = 512, 256, 512, 512, 512, 512, 1024, 128, 256, 512
FLOPS = 2 * K * R * J + 2 * Z * R * J + 2 * R * N * O

F32 = mybir.dt.float32
BF16 = mybir.dt.bfloat16
I32 = mybir.dt.int32
U32 = mybir.dt.uint32
U16 = mybir.dt.uint16
U8 = mybir.dt.uint8
FP8X4 = mybir.dt.float8_e4m3fn_x4
FP4X4 = mybir.dt.float4_e2m1fn_x4
COPY = mybir.ActivationFunctionType.Copy
MAX = mybir.AluOpType.max

P = 128
PACK = 4
HALF = J // 2


def tile_picked_codepage_plain_two_groupmeet_codes_plain_kernel(
    tc, ta, ga, gb, w_words, w_scales, xo_words, xo_scales, w2_words, w2_scales, sa, sb, va, ea,
    offs, offs2, offs3, offs4, offs5, offs6, offs7, out,
):
    nc = tc.nc
    with ExitStack() as ctx:
        lists = ctx.enter_context(tc.tile_pool(name="lists", bufs=1))
        keep = ctx.enter_context(tc.tile_pool(name="keep", bufs=1))
        shared = ctx.enter_context(tc.tile_pool(name="shared", bufs=1))
        psum = ctx.enter_context(tc.psum_pool(name="psum", bufs=1))

        def sb_tile(shape, dtype, name, tag=None):
            return keep.tile(shape, dtype, name=name, tag=tag or name, align_bytes=64)

        def load_list(src, name):
            t = lists.tile(list(src.shape), U16, name=name)
            nc.sync.dma_start(t[:], src)
            return t

        def load_column(queue, src, name):
            t = sb_tile([P, PACK], F32, name)
            queue.dma_start(t[:], src.rearrange("(p t) one -> p (t one)", t=PACK))
            return t

        def load_rows(src, t, name):
            tl = sb_tile([P, src.shape[1]], F32, name)
            nc.sync.dma_start(tl[:], src.rearrange("(p t) c -> t p c", t=PACK)[t])
            return tl

        def load_scale_rows(queue, src, plane):
            rows = src[0].bitcast(I32).rearrange("(q i) c -> i q c", i=4)
            for i in range(4):
                queue.dma_start(plane[i:P:32, :].bitcast(I32), rows[i])

        def interleave(engine, dst, src):
            engine.tensor_copy(
                dst.rearrange("p (c i) t -> p c t i", i=4),
                src.rearrange("p t (c i) -> p c t i", i=4),
            )

        warm_in = sb_tile([P, 1], F32, "warm_in")
        warm_out = sb_tile([P, 1], F32, "warm_out")
        nc.gpsimd.memset(warm_in[:], 0.0)
        nc.scalar.activation(out=warm_out[:], in_=warm_in[:], func=COPY)

        xo_plane = sb_tile([P, M], U8, "xo_plane")
        nc.vector.memset(xo_plane[:].bitcast(I32), 0)
        page = [sb_tile([P, U], F32, "page%d" % t) for t in range(PACK)]
        for t in range(PACK):
            nc.vector.memset(page[t][:], 0.0)
        w_plane = sb_tile([P, R], U8, "w_plane")
        nc.gpsimd.memset(w_plane[:].bitcast(I32), 0)
        w2_plane = sb_tile([P, R], U8, "w2_plane")
        nc.gpsimd.memset(w2_plane[:].bitcast(I32), 0)

        ta_t = [None] * PACK
        va_t = [None] * PACK
        load_scale_rows(nc.gpsimd, w_scales, w_plane)
        gb_t = load_column(nc.gpsimd, gb, "gb_t")
        xo_stage = sb_tile([4, 4, M // 4], I32, "xo_stage")
        nc.sync.dma_start(xo_stage[:], xo_scales[0].bitcast(I32).rearrange("(q i) c -> i q c", i=4))
        ta_t[0] = load_rows(ta, 0, "ta0")
        l1 = load_list(offs, "l1")
        ga_t = load_column(nc.sync, ga, "ga_t")
        l4 = load_list(offs4, "l4")
        l2 = load_list(offs2, "l2")
        ta_t[1] = load_rows(ta, 1, "ta1")
        ta_t[2] = load_rows(ta, 2, "ta2")
        va_t[0] = load_rows(va, 0, "va0")
        l7 = load_list(offs7, "l7")
        ea_t = load_column(nc.sync, ea, "ea_t")
        ta_t[3] = load_rows(ta, 3, "ta3")
        va_t[1] = load_rows(va, 1, "va1")
        w_w = sb_tile([P, R], U16, "w_w")
        nc.sync.dma_start(w_w[:].bitcast(I32), w_words[0].bitcast(I32))
        va_t[2] = load_rows(va, 2, "va2")
        va_t[3] = load_rows(va, 3, "va3")
        l3 = load_list(offs3, "l3")
        w2_w = sb_tile([P, R], U32, "w2_w")
        nc.sync.dma_start(w2_w[:].bitcast(I32), w2_words[0].rearrange("p n t -> p (n t)").bitcast(I32))
        load_scale_rows(nc.sync, w2_scales, w2_plane)
        xo_w = shared.tile([P, M], U16, name="xo_w", align_bytes=64, offset=0)
        nc.sync.dma_start(xo_w[:].bitcast(I32), xo_words[0].bitcast(I32))
        l6 = load_list(offs6, "l6")
        sb_t = load_column(nc.sync, sb, "sb_t")
        l5 = load_list(offs5, "l5")
        sa_t = load_column(nc.sync, sa, "sa_t")

        for q in range(4):
            nc.vector.tensor_copy(xo_plane[32 * q : 32 * q + 4, :].bitcast(I32), xo_stage[:, q, :])
        xo_gs = sb_tile([P, J], U8, "xo_gs")
        nc.vector.tensor_copy(xo_gs[:], xo_plane[:].indirect(l4[:]))

        w2_dw = sb_tile([P, R], U32, "w2_dw")
        nc.gpsimd.tensor_copy(w2_dw[:].rearrange("p (t m) -> p t m", t=PACK), w2_w[:].rearrange("p (m t) -> p t m", t=PACK))
        w2_ds = sb_tile([P, R], U8, "w2_ds")
        nc.gpsimd.tensor_copy(w2_ds[:].rearrange("p (t m) -> p t m", t=PACK), w2_plane[:].rearrange("p (m t) -> p t m", t=PACK))
        w_ds = sb_tile([P, R], U8, "w_ds")
        nc.gpsimd.tensor_copy(w_ds[:].rearrange("p (t m) -> p t m", t=PACK), w_plane[:].rearrange("p (m t) -> p t m", t=PACK))

        xcd = [sb_tile([P, J], F32, "xcd%d" % t) for t in range(PACK)]
        vc_pl = sb_tile([P, PACK, N], BF16, "vc_pl")
        xo_gw = sb_tile([P, J], U16, "xo_gw")

        def fetch(dst, window, lst, scale):
            nc.scalar.activation(out=dst, in_=window[:].indirect(lst), func=COPY, scale=scale)

        for t in range(PACK):
            fetch(xcd[t][:], ta_t[t], l1[:], ga_t[:, t : t + 1])
            nc.vector.tensor_copy(page[t][:].indirect(l2[:]), xcd[t][:])

        last = PACK - 1
        for t in range(PACK):
            fetch(vc_pl[:, t, :], va_t[t], l7[:], ea_t[:, t : t + 1])

        for h in range(2):
            cols = slice(h * HALF, (h + 1) * HALF)
            lcols = slice(h * HALF // 16, (h + 1) * HALF // 16)
            nc.vector.tensor_copy(xo_gw[:, cols], xo_w[:].indirect(l4[:, lcols]))

        w_dw = sb_tile([P, R], U16, "w_dw")
        nc.scalar.copy(w_dw[:].rearrange("p (t c i) -> p c t i", t=PACK, i=8), w_w[:].rearrange("p (c i t) -> p c t i", t=PACK, i=8))

        xc_pl = sb_tile([P, PACK, J], BF16, "xc_pl")
        for t in range(last):
            fetch(xc_pl[:, t, :], page[t], l3[:], gb_t[:, t : t + 1])
        xc_il = shared.tile([P, J, PACK], BF16, name="xc_il", align_bytes=64, offset=0)
        xc_q = sb_tile([P, J], U32, "xc_q")
        xc_s = sb_tile([P, J], U8, "xc_s")
        for h in range(2):
            cols = slice(h * HALF, (h + 1) * HALF)
            lcols = slice(h * HALF // 16, (h + 1) * HALF // 16)
            fetch(xc_pl[:, last, cols], page[last], l3[:, lcols], gb_t[:, last : last + 1])
            interleave(nc.vector, xc_il[:, cols, :], xc_pl[:, :, cols])
        for h in range(2):
            cols = slice(h * HALF, (h + 1) * HALF)
            nc.vector.quantize_mx(
                out=xc_q[:, cols].bitcast(FP8X4), scales=xc_s[:, cols],
                in_=xc_il[:, cols, :].rearrange("p c t -> p (c t)"),
            )

        b_sb = [sb_tile([P, J], F32, "b%d" % t) for t in range(2)]
        for t in range(2, PACK):
            b_sb.append(shared.tile([P, J], F32, name="b%d" % t, align_bytes=64, offset=1024 * (t - 2)))
        b_ps = [psum.tile([P, J], F32, name="b_ps%d" % t, tag="bank%d" % t) for t in range(PACK)]
        for h in range(2):
            cols = slice(h * HALF, (h + 1) * HALF)
            for t in range(PACK):
                rows = slice(t * P, (t + 1) * P)
                nc.tensor.matmul_mx(
                    out=b_ps[t][:, cols], lhsT=w2_dw[:, rows].bitcast(FP8X4), lhsT_scale=w2_ds[:, rows],
                    rhs=xo_gw[:, cols].bitcast(FP4X4), rhs_scale=xo_gs[:, cols], start=True, stop=True,
                )
        for t in range(PACK):
            if t < 2:
                nc.scalar.copy(b_sb[t][:], b_ps[t][:])
            else:
                nc.vector.tensor_copy(b_sb[t][:], b_ps[t][:])

        b_g = sb_tile([P, PACK, O], F32, "b_g", tag="page3")
        for t in range(PACK):
            fetch(b_g[:, t, :], b_sb[t], l6[:], sb_t[:, t : t + 1])

        a_ps = [psum.tile([P, J], F32, name="a_ps%d" % t, tag="bank%d" % (PACK + t)) for t in range(PACK)]
        a_sb = [sb_tile([P, J], F32, "a%d" % t) for t in range(PACK)]
        a_g = sb_tile([P, PACK, O], F32, "a_g")
        for t in range(PACK):
            for h in range(2):
                cols = slice(h * HALF, (h + 1) * HALF)
                nc.tensor.matmul_mx(
                    out=a_ps[t][:, cols], lhsT=w_dw[:, t * P : (t + 1) * P].bitcast(FP4X4),
                    lhsT_scale=w_ds[:, t * P : (t + 1) * P],
                    rhs=xc_q[:, cols].bitcast(FP8X4), rhs_scale=xc_s[:, cols], start=True, stop=True,
                )
            nc.vector.tensor_copy(a_sb[t][:], a_ps[t][:])
            fetch(a_g[:, t, :], a_sb[t], l5[:], sa_t[:, t : t + 1])

        vc_il = sb_tile([P, N, PACK], BF16, "vc_il", tag="xc_q")
        interleave(nc.vector, vc_il[:], vc_pl[:])

        hid_il = sb_tile([P, O, PACK], BF16, "hid_il")
        nc.vector.tensor_tensor(
            hid_il[:].rearrange("p (c i) t -> p c t i", i=4),
            a_g[:].rearrange("p t (c i) -> p c t i", i=4),
            b_g[:].rearrange("p t (c i) -> p c t i", i=4),
            MAX,
        )
        vc_q = sb_tile([P, N], U32, "vc_q")
        vc_s = sb_tile([P, N], U8, "vc_s")
        nc.vector.quantize_mx(out=vc_q[:].bitcast(FP8X4), scales=vc_s[:], in_=vc_il[:].rearrange("p c t -> p (c t)"))
        hid_q = sb_tile([P, O], U32, "hid_q")
        hid_s = sb_tile([P, O], U8, "hid_s")
        nc.vector.quantize_mx(out=hid_q[:].bitcast(FP8X4), scales=hid_s[:], in_=hid_il[:].rearrange("p c t -> p (c t)"))

        y_sb = sb_tile([P, 2, O], F32, "y_sb")
        for h in range(2):
            cols = slice(h * P, (h + 1) * P)
            y_ps = psum.tile([P, O], F32, name="y_ps%d" % h, tag="bank%d" % h)
            nc.tensor.matmul_mx(
                out=y_ps[:], lhsT=vc_q[:, cols].bitcast(FP8X4), lhsT_scale=vc_s[:, cols],
                rhs=hid_q[:].bitcast(FP8X4), rhs_scale=hid_s[:], start=True, stop=True,
            )
            if h == 0:
                nc.vector.tensor_copy(y_sb[:, h, :], y_ps[:])
            else:
                nc.scalar.copy(y_sb[:, h, :], y_ps[:])
        nc.sync.dma_start(out.rearrange("(h p) o -> p h o", p=P), y_sb[:])
